import numpy as np
import ml_dtypes


def mxq(x, axis, fmt="e4m3"):
    dtype, down = {"e4m3": (ml_dtypes.float8_e4m3fn, 7), "e5m2": (ml_dtypes.float8_e5m2, 14)}[fmt]
    v = np.moveaxis(np.asarray(x, np.float32).astype(ml_dtypes.bfloat16).astype(np.float64), axis, -1)
    blocks = v.reshape(v.shape[:-1] + (-1, 32))
    amax = np.abs(blocks).max(-1, keepdims=True)
    byte = np.maximum(np.where(amax > 0, np.frexp(amax)[1] - 1 + 127, 0) - down, 1)
    scale = np.exp2(byte - 127.0)
    codes = (blocks / scale).astype(np.float32).astype(dtype).astype(np.float64)
    return np.moveaxis((codes * scale).reshape(v.shape), -1, axis)


WIDE = False


def mx_kscale(k):
    if not WIDE:
        return np.ones(k)
    levels = np.array([10, -10, 5, -5, 0])
    if k % 512:
        return np.exp2(np.random.permutation(np.resize(levels, k // 32))).repeat(32)
    a = np.empty((k // 512, 16))
    for p in range(k // 512):
        a[p, :8] = np.random.permutation(np.resize(levels, 8))
        for g in range(8):
            far = levels[np.abs(levels - a[p, g]) >= 10]
            a[p, g + 8] = far[np.random.randint(len(far))]
    return np.exp2(a.ravel()).repeat(32)


def f64(x):
    return np.asarray(x).astype(np.float64)


def striped8(idx):
    return np.asarray(idx).reshape(8, -1, 16).transpose(0, 2, 1).reshape(128, -1).astype(np.uint16)


def unstriped8(offs):
    return offs.reshape(8, 16, -1).transpose(0, 2, 1).reshape(8, -1).astype(np.int64)


def pick8(x, idx, run):
    r = np.arange(len(x))
    return x[r[:, None], idx[r % (8 * run) // run]]


E2M1 = np.array([0.0, 0.5, 1.0, 1.5, 2.0, 3.0, 4.0, 6.0, -0.0, -0.5, -1.0, -1.5, -2.0, -3.0, -4.0, -6.0])


def pack_weight(w, fmt):
    k, n = w.shape
    w = f64(np.asarray(w, np.float32).astype(ml_dtypes.bfloat16)).reshape(k // 32, 32, n)
    amax = np.abs(w).max(1)
    if fmt == "e4m3":
        byte = np.frexp(amax)[1] - 1 + 127 - 7
    else:
        mant, ex = np.frexp(amax / 6.0)
        byte = np.where(mant > 0.5, ex, ex - 1) + 127
    byte = np.clip(np.where(amax > 0, byte, 1), 1, 254)
    scaled = (w * np.exp2(127.0 - byte)[:, None, :]).reshape(k, n).astype(np.float32)
    by_word = np.ascontiguousarray(scaled.reshape(k // 512, 128, 4, n).transpose(0, 1, 3, 2))
    if fmt == "e4m3":
        words = by_word.astype(ml_dtypes.float8_e4m3fn).view(np.uint8)
    else:
        c = by_word.astype(ml_dtypes.float4_e2m1fn).view(np.uint8) & 0xF
        words = (c[..., 0::2] | (c[..., 1::2] << 4)).reshape(k // 512, 128, 2 * n)
    return np.ascontiguousarray(words), np.ascontiguousarray(byte.astype(np.uint8).reshape(k // 512, 16, n))


def unpack_weight(words, scales, fmt):
    g, _, n = scales.shape
    words = np.ascontiguousarray(words).reshape(g, 128, n, -1)
    if fmt == "e4m3":
        vals = words.view(ml_dtypes.float8_e4m3fn).astype(np.float64)
    else:
        nib = np.empty((g, 128, n, 4), np.uint8)
        nib[..., 0::2] = words & 0xF
        nib[..., 1::2] = words >> 4
        vals = E2M1[nib]
    vals = vals * np.repeat(np.exp2(scales.astype(np.float64) - 127.0), 8, axis=1)[..., None]
    return vals.transpose(0, 1, 3, 2).reshape(g * 512, n)


D, K, T, U, I, Q = 512, 512, 1024, 1024, 512, 128


def setup_inputs():
    n = np.random.standard_normal
    idx = np.stack([np.random.permutation(T)[:I] for _ in range(8)])
    idx2 = np.stack([np.random.permutation(U)[:I] for _ in range(8)])
    idx3 = np.stack([np.random.permutation(U)[:I] for _ in range(8)])
    idx4 = np.stack([np.random.permutation(T)[:I] for _ in range(8)])
    fd = mx_kscale(D)
    fk = mx_kscale(K)
    wqp = pack_weight(n((D, K)) * 1.0 / np.sqrt(D) * fd[:, None] * fk, "e4m3")
    keysp = pack_weight(n((K, T)) * 1.0 / np.sqrt(K) / fk[:, None], "e2m1")
    notesp = pack_weight(n((D, U)) * 1.0 / np.sqrt(D) * fd[:, None], "e4m3")
    return {
        "states": (n((D, Q)) * 0.95 / fd[:, None]).astype(np.float32),
        "wq_words": wqp[0],
        "wq_scales": wqp[1],
        "keys_words": keysp[0],
        "keys_scales": keysp[1],
        "notes_words": notesp[0],
        "notes_scales": notesp[1],
        "lam": (np.random.uniform(0.5, 1.5, (Q, 1))).astype(np.float32),
        "offs": striped8(idx),
        "offs2": striped8(idx2),
        "offs3": striped8(idx3),
        "offs4": striped8(idx4),
    }


def reference(states, wq_words, wq_scales, keys_words, keys_scales, notes_words, notes_scales, lam, offs, offs2, offs3, offs4):
    idx = unstriped8(offs)
    idx2 = unstriped8(offs2)
    idx3 = unstriped8(offs3)
    idx4 = unstriped8(offs4)
    wqu = unpack_weight(wq_words, wq_scales, "e4m3")
    keysu = unpack_weight(keys_words, keys_scales, "e2m1")
    notesu = unpack_weight(notes_words, notes_scales, "e4m3")
    statesq = mxq(f64(states), 0, "e4m3")
    qv = wqu.T @ statesq
    qvq = mxq(qv, 0, "e4m3")
    a = qvq.T @ keysu
    b = statesq.T @ notesu
    w = pick8(a, idx, 16) - pick8(b, idx2, 16)
    f1 = np.zeros((Q, U))
    f1[np.arange(Q)[:, None], idx3[np.arange(Q) % 128 // 16]] = w
    bb = b + f1 * f64(lam)
    y = pick8(bb, idx2, 16) + pick8(a, idx4, 16)
    return y

@@ -1,0 +1,163 @@
+from contextlib import ExitStack
+
+import concourse.mybir as mybir
+
+F32 = mybir.dt.float32
+BF16 = mybir.dt.bfloat16
+I32 = mybir.dt.int32
+U32 = mybir.dt.uint32
+U16 = mybir.dt.uint16
+U8 = mybir.dt.uint8
+FP8X4 = mybir.dt.float8_e4m3fn_x4
+FP4X4 = mybir.dt.float4_e2m1fn_x4
+ALU = mybir.AluOpType
+COPY = mybir.ActivationFunctionType.Copy
+
+P = 128
+PACK = 4
+D, K, T, U, SLOTS, Q = 512, 512, 1024, 1024, 512, 128
+CHUNK = 256
+HALF = SLOTS // 2
+LIST_COLS = SLOTS // 16
+
+FLOPS = 2 * (D * K * Q + K * Q * T + D * Q * U)
+
+
+def load_scale_rows(queues, plane, scales):
+    for quad in range(4):
+        queues[quad].dma_start(
+            out=plane[32 * quad : 32 * quad + 4, :].bitcast(I32),
+            in_=scales[0, 4 * quad : 4 * quad + 4, :].bitcast(I32),
+        )
+
+
+def tile_attend_followers_madeside_kernel(
+    tc, states, wq_words, wq_scales, keys_words, keys_scales, notes_words, notes_scales,
+    lam, offs, offs2, offs3, offs4, out,
+):
+    nc = tc.nc
+    with ExitStack() as ctx:
+        lists = ctx.enter_context(tc.tile_pool(name="lists", bufs=1))
+        sb = ctx.enter_context(tc.tile_pool(name="sb", bufs=1))
+        psum = ctx.enter_context(tc.psum_pool(name="psum", bufs=1))
+
+        wq_plane_raw = sb.tile([P, K], U8, align_bytes=64)
+        notes_plane = sb.tile([P, U], U8, align_bytes=64)
+        keys_plane = sb.tile([P, T], U8, align_bytes=64)
+        nc.vector.memset(wq_plane_raw[:].bitcast(I32), 0)
+        nc.vector.memset(notes_plane[:].bitcast(I32), 0)
+        nc.vector.memset(keys_plane[:].bitcast(I32), 0)
+
+        states_raw = sb.tile([P, PACK, Q], F32, align_bytes=64)
+        wq_raw = sb.tile([P, K], U32, align_bytes=64, tag="wq_raw_then_f1")
+        notes_codes = sb.tile([P, U], U32, align_bytes=64)
+        keys_codes = sb.tile([P, 2 * T], U8, align_bytes=64)
+        tok_list = lists.tile([P, LIST_COLS], U16)
+        note_list = lists.tile([P, LIST_COLS], U16)
+        place_list = lists.tile([P, LIST_COLS], U16)
+        tok2_list = lists.tile([P, LIST_COLS], U16)
+        lam_col = sb.tile([P, 1], F32)
+
+        nc.sync.dma_start(out=states_raw[:], in_=states.rearrange("(p j) q -> p j q", j=PACK))
+        nc.sync.dma_start(out=wq_raw[:].bitcast(I32), in_=wq_words[0].rearrange("p n t -> p (n t)").bitcast(I32))
+        load_scale_rows([nc.scalar] * 4, wq_plane_raw, wq_scales)
+        nc.sync.dma_start(note_list[:], offs2)
+        nc.sync.dma_start(out=notes_codes[:].bitcast(I32), in_=notes_words[0].rearrange("p n t -> p (n t)").bitcast(I32))
+        load_scale_rows([nc.gpsimd, nc.gpsimd, nc.sync, nc.sync], notes_plane, notes_scales)
+        nc.sync.dma_start(out=keys_codes[:].bitcast(I32), in_=keys_words[0].bitcast(I32))
+        load_scale_rows([nc.gpsimd, nc.sync, nc.sync, nc.sync], keys_plane, keys_scales)
+        nc.sync.dma_start(tok_list[:], offs)
+        nc.sync.dma_start(place_list[:], offs3)
+        nc.sync.dma_start(tok2_list[:], offs4)
+        nc.sync.dma_start(out=lam_col[:], in_=lam)
+
+        wq_plane = sb.tile([P, PACK, P], U8, align_bytes=64)
+        nc.vector.tensor_copy(out=wq_plane[:], in_=wq_plane_raw[:].rearrange("p (m j) -> p j m", j=PACK))
+        wq_codes = sb.tile([P, PACK, P], U32, align_bytes=64)
+        nc.scalar.copy(
+            out=wq_codes[:].rearrange("p j (c i) -> p c j i", i=4),
+            in_=wq_raw[:].rearrange("p (c i j) -> p c j i", i=4, j=PACK),
+        )
+
+        states_bf = sb.tile([P, Q, PACK], BF16, align_bytes=64)
+        nc.vector.tensor_copy(
+            out=states_bf[:].rearrange("p (c i) j -> p c i j", i=4),
+            in_=states_raw[:].rearrange("p j (c i) -> p c i j", i=4),
+        )
+        states_codes = sb.tile([P, Q], U32, align_bytes=64)
+        states_plane = sb.tile([P, Q], U8, align_bytes=64)
+        nc.vector.quantize_mx(
+            out=states_codes[:].bitcast(FP8X4), scales=states_plane[:],
+            in_=states_bf[:].rearrange("p q j -> p (q j)"),
+        )
+
+        qv_ps = psum.tile([P, PACK, Q], F32, tag="qv")
+        for j in range(PACK):
+            nc.tensor.matmul_mx(
+                out=qv_ps[:, j, :], lhsT=wq_codes[:, j, :].bitcast(FP8X4), lhsT_scale=wq_plane[:, j, :],
+                rhs=states_codes[:].bitcast(FP8X4), rhs_scale=states_plane[:], start=True, stop=True,
+            )
+        qv_bf = sb.tile([P, Q, PACK], BF16, align_bytes=64)
+        nc.scalar.copy(out=qv_bf[:], in_=qv_ps[:].rearrange("p j q -> p q j"))
+        qv_codes = sb.tile([P, Q], U32, align_bytes=64)
+        qv_plane = sb.tile([P, Q], U8, align_bytes=64)
+        nc.vector.quantize_mx(
+            out=qv_codes[:].bitcast(FP8X4), scales=qv_plane[:],
+            in_=qv_bf[:].rearrange("p q j -> p (q j)"),
+        )
+
+        b = sb.tile([P, U], F32)
+        for c in range(U // CHUNK):
+            cols = slice(c * CHUNK, (c + 1) * CHUNK)
+            bank = psum.tile([P, CHUNK], F32, tag="b%d" % c, name="b_ps%d" % c)
+            nc.tensor.matmul_mx(
+                out=bank[:], lhsT=states_codes[:].bitcast(FP8X4), lhsT_scale=states_plane[:],
+                rhs=notes_codes[:, cols].bitcast(FP8X4), rhs_scale=notes_plane[:, cols], start=True, stop=True,
+            )
+            if c in (0, 3):
+                nc.vector.tensor_copy(out=b[:, cols], in_=bank[:])
+            else:
+                nc.scalar.copy(out=b[:, cols], in_=bank[:])
+
+        neg_b_listed = sb.tile([P, SLOTS], F32)
+        nc.vector.tensor_scalar(
+            neg_b_listed[:, :HALF], b[:].indirect(note_list[:, : LIST_COLS // 2]), -1.0, 0.0, ALU.mult, ALU.add
+        )
+        nc.scalar.activation(neg_b_listed[:, HALF:], b[:].indirect(note_list[:, LIST_COLS // 2 :]), COPY, scale=-1.0)
+
+        a = sb.tile([P, T], F32)
+        for c in range(T // CHUNK):
+            cols = slice(c * CHUNK, (c + 1) * CHUNK)
+            bank = psum.tile([P, CHUNK], F32, tag=("a%d" % c if c < 3 else "qv"), name="a_ps%d" % c)
+            nc.tensor.matmul_mx(
+                out=bank[:], lhsT=qv_codes[:].bitcast(FP8X4), lhsT_scale=qv_plane[:],
+                rhs=keys_codes[:, 2 * c * CHUNK : 2 * (c + 1) * CHUNK].bitcast(FP4X4), rhs_scale=keys_plane[:, cols],
+                start=True, stop=True,
+            )
+            if c % 2 == 0:
+                nc.vector.tensor_copy(out=a[:, cols], in_=bank[:])
+            else:
+                nc.scalar.copy(out=a[:, cols], in_=bank[:])
+
+        a_listed = sb.tile([P, SLOTS], F32)
+        nc.vector.tensor_copy(a_listed[:, :HALF], a[:].indirect(tok_list[:, : LIST_COLS // 2]))
+        nc.scalar.activation(a_listed[:, HALF:], a[:].indirect(tok_list[:, LIST_COLS // 2 :]), COPY)
+
+        f1 = sb.tile([P, U], F32, align_bytes=64, tag="wq_raw_then_f1")
+        nc.vector.memset(f1[:], 0.0)
+        nc.vector.tensor_tensor(f1[:].indirect(place_list[:]), a_listed[:], neg_b_listed[:], ALU.add)
+
+        a_listed2 = sb.tile([P, SLOTS], F32)
+        nc.scalar.activation(a_listed2[:], a[:].indirect(tok2_list[:]), COPY)
+
+        bb = sb.tile([P, U], F32)
+        nc.vector.scalar_tensor_tensor(bb[:], f1[:], lam_col[:], b[:], ALU.mult, ALU.add)
+
+        res_lo = sb.tile([P, HALF], F32)
+        nc.vector.tensor_tensor(res_lo[:], bb[:].indirect(note_list[:, : LIST_COLS // 2]), a_listed2[:, :HALF], ALU.add)
+        nc.sync.dma_start(out=out[:, :HALF], in_=res_lo[:])
+        bb_hi = sb.tile([P, HALF], F32)
+        nc.scalar.activation(bb_hi[:], bb[:].indirect(note_list[:, LIST_COLS // 2 :]), COPY)
+        res_hi = sb.tile([P, HALF], F32)
+        nc.vector.tensor_tensor(res_hi[:], bb_hi[:], a_listed2[:, HALF:], ALU.add)
+        nc.sync.dma_start(out=out[:, HALF:], in_=res_hi[:])

@@ -45,27 +45,27 @@ def tile_attend_followers_madeside_kernel(
         notes_plane = sb.tile([P, U], U8, align_bytes=64)
         keys_plane = sb.tile([P, T], U8, align_bytes=64)
         nc.vector.memset(wq_plane_raw[:].bitcast(I32), 0)
-        nc.vector.memset(notes_plane[:].bitcast(I32), 0)
+        nc.gpsimd.memset(notes_plane[:].bitcast(I32), 0)
         nc.vector.memset(keys_plane[:].bitcast(I32), 0)
 
         states_raw = sb.tile([P, PACK, Q], F32, align_bytes=64)
         wq_raw = sb.tile([P, K], U32, align_bytes=64, tag="wq_raw_then_f1")
         notes_codes = sb.tile([P, U], U32, align_bytes=64)
-        keys_codes = sb.tile([P, 2 * T], U8, align_bytes=64)
+        keys_codes = sb.tile([P, 2 * T], U8, align_bytes=64, tag="keys_codes_then_neg_b")
         tok_list = lists.tile([P, LIST_COLS], U16)
         note_list = lists.tile([P, LIST_COLS], U16)
         place_list = lists.tile([P, LIST_COLS], U16)
         tok2_list = lists.tile([P, LIST_COLS], U16)
         lam_col = sb.tile([P, 1], F32)
 
-        nc.sync.dma_start(out=states_raw[:], in_=states.rearrange("(p j) q -> p j q", j=PACK))
         nc.sync.dma_start(out=wq_raw[:].bitcast(I32), in_=wq_words[0].rearrange("p n t -> p (n t)").bitcast(I32))
-        load_scale_rows([nc.scalar] * 4, wq_plane_raw, wq_scales)
+        nc.sync.dma_start(out=states_raw[:], in_=states.rearrange("(p j) q -> p j q", j=PACK))
+        load_scale_rows([nc.scalar, nc.scalar, nc.scalar, nc.scalar], wq_plane_raw, wq_scales)
+        nc.gpsimd.dma_start(out=notes_codes[:].bitcast(I32), in_=notes_words[0].rearrange("p n t -> p (n t)").bitcast(I32))
+        nc.gpsimd.dma_start(out=keys_codes[:].bitcast(I32), in_=keys_words[0].bitcast(I32))
+        load_scale_rows([nc.sync, nc.sync, nc.sync, nc.sync], notes_plane, notes_scales)
+        load_scale_rows([nc.sync, nc.sync, nc.sync, nc.sync], keys_plane, keys_scales)
         nc.sync.dma_start(note_list[:], offs2)
-        nc.sync.dma_start(out=notes_codes[:].bitcast(I32), in_=notes_words[0].rearrange("p n t -> p (n t)").bitcast(I32))
-        load_scale_rows([nc.gpsimd, nc.gpsimd, nc.sync, nc.sync], notes_plane, notes_scales)
-        nc.sync.dma_start(out=keys_codes[:].bitcast(I32), in_=keys_words[0].bitcast(I32))
-        load_scale_rows([nc.gpsimd, nc.sync, nc.sync, nc.sync], keys_plane, keys_scales)
         nc.sync.dma_start(tok_list[:], offs)
         nc.sync.dma_start(place_list[:], offs3)
         nc.sync.dma_start(tok2_list[:], offs4)
@@ -107,28 +107,18 @@ def tile_attend_followers_madeside_kernel(
         )
 
         b = sb.tile([P, U], F32)
-        for c in range(U // CHUNK):
-            cols = slice(c * CHUNK, (c + 1) * CHUNK)
-            bank = psum.tile([P, CHUNK], F32, tag="b%d" % c, name="b_ps%d" % c)
+        for lo, hi, tag, copy in ((0, 512, "b0", nc.scalar.copy), (512, 768, "b1", nc.scalar.copy), (768, 1024, "qv", nc.vector.tensor_copy)):
+            bank = psum.tile([P, hi - lo], F32, tag=tag, name="b_ps%d" % lo)
             nc.tensor.matmul_mx(
                 out=bank[:], lhsT=states_codes[:].bitcast(FP8X4), lhsT_scale=states_plane[:],
-                rhs=notes_codes[:, cols].bitcast(FP8X4), rhs_scale=notes_plane[:, cols], start=True, stop=True,
+                rhs=notes_codes[:, lo:hi].bitcast(FP8X4), rhs_scale=notes_plane[:, lo:hi], start=True, stop=True,
             )
-            if c in (0, 3):
-                nc.vector.tensor_copy(out=b[:, cols], in_=bank[:])
-            else:
-                nc.scalar.copy(out=b[:, cols], in_=bank[:])
-
-        neg_b_listed = sb.tile([P, SLOTS], F32)
-        nc.vector.tensor_scalar(
-            neg_b_listed[:, :HALF], b[:].indirect(note_list[:, : LIST_COLS // 2]), -1.0, 0.0, ALU.mult, ALU.add
-        )
-        nc.scalar.activation(neg_b_listed[:, HALF:], b[:].indirect(note_list[:, LIST_COLS // 2 :]), COPY, scale=-1.0)
+            copy(out=b[:, lo:hi], in_=bank[:])
 
         a = sb.tile([P, T], F32)
         for c in range(T // CHUNK):
             cols = slice(c * CHUNK, (c + 1) * CHUNK)
-            bank = psum.tile([P, CHUNK], F32, tag=("a%d" % c if c < 3 else "qv"), name="a_ps%d" % c)
+            bank = psum.tile([P, CHUNK], F32, tag="a%d" % c, name="a_ps%d" % c)
             nc.tensor.matmul_mx(
                 out=bank[:], lhsT=qv_codes[:].bitcast(FP8X4), lhsT_scale=qv_plane[:],
                 rhs=keys_codes[:, 2 * c * CHUNK : 2 * (c + 1) * CHUNK].bitcast(FP4X4), rhs_scale=keys_plane[:, cols],
@@ -139,13 +129,18 @@ def tile_attend_followers_madeside_kernel(
             else:
                 nc.scalar.copy(out=a[:, cols], in_=bank[:])
 
-        a_listed = sb.tile([P, SLOTS], F32)
-        nc.vector.tensor_copy(a_listed[:, :HALF], a[:].indirect(tok_list[:, : LIST_COLS // 2]))
-        nc.scalar.activation(a_listed[:, HALF:], a[:].indirect(tok_list[:, LIST_COLS // 2 :]), COPY)
-
         f1 = sb.tile([P, U], F32, align_bytes=64, tag="wq_raw_then_f1")
         nc.vector.memset(f1[:], 0.0)
-        nc.vector.tensor_tensor(f1[:].indirect(place_list[:]), a_listed[:], neg_b_listed[:], ALU.add)
+        neg_b_listed = sb.tile([P, SLOTS], F32, align_bytes=64, tag="keys_codes_then_neg_b")
+        a_listed = sb.tile([P, SLOTS], F32)
+        halves = [(slice(h * HALF, (h + 1) * HALF), slice(h * HALF // 16, (h + 1) * HALF // 16)) for h in range(2)]
+        for slots, list_cols in halves:
+            nc.vector.tensor_scalar(
+                neg_b_listed[:, slots], b[:].indirect(note_list[:, list_cols]), -1.0, 0.0, ALU.mult, ALU.add
+            )
+            nc.scalar.activation(a_listed[:, slots], a[:].indirect(tok_list[:, list_cols]), COPY)
+        for slots, list_cols in halves:
+            nc.vector.tensor_tensor(f1[:].indirect(place_list[:, list_cols]), a_listed[:, slots], neg_b_listed[:, slots], ALU.add)
 
         a_listed2 = sb.tile([P, SLOTS], F32)
         nc.scalar.activation(a_listed2[:], a[:].indirect(tok2_list[:]), COPY)

@@ -71,6 +71,13 @@ def tile_attend_followers_madeside_kernel(
         nc.sync.dma_start(tok2_list[:], offs4)
         nc.sync.dma_start(out=lam_col[:], in_=lam)
 
+        warm = psum.tile([32, K], F32, tag="warm")
+        for rep in range(2):
+            nc.tensor.matmul_mx(
+                out=warm[:], lhsT=wq_raw[:, :32].bitcast(FP8X4), lhsT_scale=wq_plane_raw[:, :32],
+                rhs=wq_raw[:].bitcast(FP8X4), rhs_scale=wq_plane_raw[:], start=True, stop=True,
+            )
+
         wq_plane = sb.tile([P, PACK, P], U8, align_bytes=64)
         nc.vector.tensor_copy(out=wq_plane[:], in_=wq_plane_raw[:].rearrange("p (m j) -> p j m", j=PACK))
         wq_codes = sb.tile([P, PACK, P], U32, align_bytes=64)

from contextlib import ExitStack

import concourse.mybir as mybir

F32 = mybir.dt.float32
BF16 = mybir.dt.bfloat16
I32 = mybir.dt.int32
U32 = mybir.dt.uint32
U16 = mybir.dt.uint16
U8 = mybir.dt.uint8
FP8X4 = mybir.dt.float8_e4m3fn_x4
FP4X4 = mybir.dt.float4_e2m1fn_x4
ALU = mybir.AluOpType
COPY = mybir.ActivationFunctionType.Copy

P = 128
PACK = 4
D, K, T, U, SLOTS, Q = 512, 512, 1024, 1024, 512, 128
CHUNK = 256
HALF = SLOTS // 2
LIST_COLS = SLOTS // 16

FLOPS = 2 * (D * K * Q + K * Q * T + D * Q * U)


def load_scale_rows(queues, plane, scales):
    for quad in range(4):
        queues[quad].dma_start(
            out=plane[32 * quad : 32 * quad + 4, :].bitcast(I32),
            in_=scales[0, 4 * quad : 4 * quad + 4, :].bitcast(I32),
        )


def tile_attend_followers_madeside_kernel(
    tc, states, wq_words, wq_scales, keys_words, keys_scales, notes_words, notes_scales,
    lam, offs, offs2, offs3, offs4, out,
):
    nc = tc.nc
    with ExitStack() as ctx:
        lists = ctx.enter_context(tc.tile_pool(name="lists", bufs=1))
        sb = ctx.enter_context(tc.tile_pool(name="sb", bufs=1))
        psum = ctx.enter_context(tc.psum_pool(name="psum", bufs=1))

        wq_plane_raw = sb.tile([P, K], U8, align_bytes=64)
        notes_plane = sb.tile([P, U], U8, align_bytes=64)
        keys_plane = sb.tile([P, T], U8, align_bytes=64)
        nc.vector.memset(wq_plane_raw[:].bitcast(I32), 0)
        nc.gpsimd.memset(notes_plane[:].bitcast(I32), 0)
        nc.vector.memset(keys_plane[:].bitcast(I32), 0)

        states_raw = sb.tile([P, PACK, Q], F32, align_bytes=64)
        wq_raw = sb.tile([P, K], U32, align_bytes=64, tag="wq_raw_then_f1")
        notes_codes = sb.tile([P, U], U32, align_bytes=64)
        keys_codes = sb.tile([P, 2 * T], U8, align_bytes=64, tag="keys_codes_then_neg_b")
        tok_list = lists.tile([P, LIST_COLS], U16)
        note_list = lists.tile([P, LIST_COLS], U16)
        place_list = lists.tile([P, LIST_COLS], U16)
        tok2_list = lists.tile([P, LIST_COLS], U16)
        lam_col = sb.tile([P, 1], F32)

        nc.sync.dma_start(out=wq_raw[:].bitcast(I32), in_=wq_words[0].rearrange("p n t -> p (n t)").bitcast(I32))
        nc.sync.dma_start(out=states_raw[:], in_=states.rearrange("(p j) q -> p j q", j=PACK))
        load_scale_rows([nc.scalar, nc.scalar, nc.scalar, nc.scalar], wq_plane_raw, wq_scales)
        nc.gpsimd.dma_start(out=notes_codes[:].bitcast(I32), in_=notes_words[0].rearrange("p n t -> p (n t)").bitcast(I32))
        nc.gpsimd.dma_start(out=keys_codes[:].bitcast(I32), in_=keys_words[0].bitcast(I32))
        load_scale_rows([nc.sync, nc.sync, nc.sync, nc.sync], notes_plane, notes_scales)
        load_scale_rows([nc.sync, nc.sync, nc.sync, nc.sync], keys_plane, keys_scales)
        nc.sync.dma_start(note_list[:], offs2)
        nc.sync.dma_start(tok_list[:], offs)
        nc.sync.dma_start(place_list[:], offs3)
        nc.sync.dma_start(tok2_list[:], offs4)
        nc.sync.dma_start(out=lam_col[:], in_=lam)

        warm = psum.tile([32, K], F32, tag="warm")
        for rep in range(2):
            nc.tensor.matmul_mx(
                out=warm[:], lhsT=wq_raw[:, :32].bitcast(FP8X4), lhsT_scale=wq_plane_raw[:, :32],
                rhs=wq_raw[:].bitcast(FP8X4), rhs_scale=wq_plane_raw[:], start=True, stop=True,
            )

        wq_plane = sb.tile([P, PACK, P], U8, align_bytes=64)
        nc.vector.tensor_copy(out=wq_plane[:], in_=wq_plane_raw[:].rearrange("p (m j) -> p j m", j=PACK))
        wq_codes = sb.tile([P, PACK, P], U32, align_bytes=64)
        nc.scalar.copy(
            out=wq_codes[:].rearrange("p j (c i) -> p c j i", i=4),
            in_=wq_raw[:].rearrange("p (c i j) -> p c j i", i=4, j=PACK),
        )

        states_bf = sb.tile([P, Q, PACK], BF16, align_bytes=64)
        nc.vector.tensor_copy(
            out=states_bf[:].rearrange("p (c i) j -> p c i j", i=4),
            in_=states_raw[:].rearrange("p j (c i) -> p c i j", i=4),
        )
        states_codes = sb.tile([P, Q], U32, align_bytes=64)
        states_plane = sb.tile([P, Q], U8, align_bytes=64)
        nc.vector.quantize_mx(
            out=states_codes[:].bitcast(FP8X4), scales=states_plane[:],
            in_=states_bf[:].rearrange("p q j -> p (q j)"),
        )

        qv_ps = psum.tile([P, PACK, Q], F32, tag="qv")
        for j in range(PACK):
            nc.tensor.matmul_mx(
                out=qv_ps[:, j, :], lhsT=wq_codes[:, j, :].bitcast(FP8X4), lhsT_scale=wq_plane[:, j, :],
                rhs=states_codes[:].bitcast(FP8X4), rhs_scale=states_plane[:], start=True, stop=True,
            )
        qv_bf = sb.tile([P, Q, PACK], BF16, align_bytes=64)
        nc.scalar.copy(out=qv_bf[:], in_=qv_ps[:].rearrange("p j q -> p q j"))
        qv_codes = sb.tile([P, Q], U32, align_bytes=64)
        qv_plane = sb.tile([P, Q], U8, align_bytes=64)
        nc.vector.quantize_mx(
            out=qv_codes[:].bitcast(FP8X4), scales=qv_plane[:],
            in_=qv_bf[:].rearrange("p q j -> p (q j)"),
        )

        b = sb.tile([P, U], F32)
        for lo, hi, tag, copy in ((0, 512, "b0", nc.scalar.copy), (512, 768, "b1", nc.scalar.copy), (768, 1024, "qv", nc.vector.tensor_copy)):
            bank = psum.tile([P, hi - lo], F32, tag=tag, name="b_ps%d" % lo)
            nc.tensor.matmul_mx(
                out=bank[:], lhsT=states_codes[:].bitcast(FP8X4), lhsT_scale=states_plane[:],
                rhs=notes_codes[:, lo:hi].bitcast(FP8X4), rhs_scale=notes_plane[:, lo:hi], start=True, stop=True,
            )
            copy(out=b[:, lo:hi], in_=bank[:])

        a = sb.tile([P, T], F32)
        for c in range(T // CHUNK):
            cols = slice(c * CHUNK, (c + 1) * CHUNK)
            bank = psum.tile([P, CHUNK], F32, tag="a%d" % c, name="a_ps%d" % c)
            nc.tensor.matmul_mx(
                out=bank[:], lhsT=qv_codes[:].bitcast(FP8X4), lhsT_scale=qv_plane[:],
                rhs=keys_codes[:, 2 * c * CHUNK : 2 * (c + 1) * CHUNK].bitcast(FP4X4), rhs_scale=keys_plane[:, cols],
                start=True, stop=True,
            )
            if c % 2 == 0:
                nc.vector.tensor_copy(out=a[:, cols], in_=bank[:])
            else:
                nc.scalar.copy(out=a[:, cols], in_=bank[:])

        f1 = sb.tile([P, U], F32, align_bytes=64, tag="wq_raw_then_f1")
        nc.vector.memset(f1[:], 0.0)
        neg_b_listed = sb.tile([P, SLOTS], F32, align_bytes=64, tag="keys_codes_then_neg_b")
        a_listed = sb.tile([P, SLOTS], F32)
        halves = [(slice(h * HALF, (h + 1) * HALF), slice(h * HALF // 16, (h + 1) * HALF // 16)) for h in range(2)]
        for slots, list_cols in halves:
            nc.vector.tensor_scalar(
                neg_b_listed[:, slots], b[:].indirect(note_list[:, list_cols]), -1.0, 0.0, ALU.mult, ALU.add
            )
            nc.scalar.activation(a_listed[:, slots], a[:].indirect(tok_list[:, list_cols]), COPY)
        for slots, list_cols in halves:
            nc.vector.tensor_tensor(f1[:].indirect(place_list[:, list_cols]), a_listed[:, slots], neg_b_listed[:, slots], ALU.add)

        a_listed2 = sb.tile([P, SLOTS], F32)
        nc.scalar.activation(a_listed2[:], a[:].indirect(tok2_list[:]), COPY)

        bb = sb.tile([P, U], F32)
        nc.vector.scalar_tensor_tensor(bb[:], f1[:], lam_col[:], b[:], ALU.mult, ALU.add)

        res_lo = sb.tile([P, HALF], F32)
        nc.vector.tensor_tensor(res_lo[:], bb[:].indirect(note_list[:, : LIST_COLS // 2]), a_listed2[:, :HALF], ALU.add)
        nc.sync.dma_start(out=out[:, :HALF], in_=res_lo[:])
        bb_hi = sb.tile([P, HALF], F32)
        nc.scalar.activation(bb_hi[:], bb[:].indirect(note_list[:, LIST_COLS // 2 :]), COPY)
        res_hi = sb.tile([P, HALF], F32)
        nc.vector.tensor_tensor(res_hi[:], bb_hi[:], a_listed2[:, HALF:], ALU.add)
        nc.sync.dma_start(out=out[:, HALF:], in_=res_hi[:])
